import numpy as np
import ml_dtypes


def mxq(x, axis, fmt="e4m3"):
    dtype, down = {"e4m3": (ml_dtypes.float8_e4m3fn, 7), "e5m2": (ml_dtypes.float8_e5m2, 14)}[fmt]
    v = np.moveaxis(np.asarray(x, np.float32).astype(ml_dtypes.bfloat16).astype(np.float64), axis, -1)
    blocks = v.reshape(v.shape[:-1] + (-1, 32))
    amax = np.abs(blocks).max(-1, keepdims=True)
    byte = np.maximum(np.where(amax > 0, np.frexp(amax)[1] - 1 + 127, 0) - down, 1)
    scale = np.exp2(byte - 127.0)
    codes = (blocks / scale).astype(np.float32).astype(dtype).astype(np.float64)
    return np.moveaxis((codes * scale).reshape(v.shape), -1, axis)


WIDE = False


def mx_kscale(k):
    if not WIDE:
        return np.ones(k)
    levels = np.array([10, -10, 5, -5, 0])
    if k % 512:
        return np.exp2(np.random.permutation(np.resize(levels, k // 32))).repeat(32)
    a = np.empty((k // 512, 16))
    for p in range(k // 512):
        a[p, :8] = np.random.permutation(np.resize(levels, 8))
        for g in range(8):
            far = levels[np.abs(levels - a[p, g]) >= 10]
            a[p, g + 8] = far[np.random.randint(len(far))]
    return np.exp2(a.ravel()).repeat(32)


def f64(x):
    return np.asarray(x).astype(np.float64)


def striped(idx):
    return np.tile(idx.reshape(-1, 16).T, (8, 1)).astype(np.uint16)


def unstriped(offs):
    return offs[:16].T.reshape(-1).astype(np.int64)


def pack_weight(w):
    k, n = w.shape
    w = f64(np.asarray(w, np.float32).astype(ml_dtypes.bfloat16)).reshape(k // 32, 32, n)
    amax = np.abs(w).max(1)
    byte = np.clip(np.where(amax > 0, np.frexp(amax)[1] - 1 + 127 - 7, 1), 1, 254)
    scaled = (w * np.exp2(127.0 - byte)[:, None, :]).reshape(k, n).astype(np.float32)
    words = np.ascontiguousarray(scaled.reshape(k // 512, 128, 4, n).transpose(0, 1, 3, 2)).astype(ml_dtypes.float8_e4m3fn).view(np.uint8)
    return words, np.ascontiguousarray(byte.astype(np.uint8).reshape(k // 512, 16, n))


def unpack_weight(words, scales):
    g, p, n, _ = words.shape
    vals = np.ascontiguousarray(words).view(ml_dtypes.float8_e4m3fn).astype(np.float64) * np.repeat(np.exp2(scales.astype(np.float64) - 127.0), 8, axis=1)[..., None]
    return vals.transpose(0, 1, 3, 2).reshape(g * 512, n)


def relu(v):
    return np.maximum(v, 0.0)


def sigmoid(v):
    return 1.0 / (1.0 + np.exp(-np.maximum(v, -700.0)))


K, T, S, D, N, V = 512, 4096, 1024, 8, 256, 128
P = 2 ** 7


def setup_inputs():
    n = np.random.standard_normal
    s = mx_kscale(K)[:, None]
    packed_xT = pack_weight(n((K, T)) * s)
    return {
        "x_words": packed_xT[0],
        "x_scales": packed_xT[1],
        "w1": (n((K, N)) / np.sqrt(K) / s).astype(np.float32),
        "w2": (n((K, N)) / np.sqrt(K) / s).astype(np.float32),
        "mult": (np.random.uniform(0.5, 2.0, (N, V))).astype(np.float32),
        "budg": (np.tile(np.random.uniform(0.1, 0.7, V), (P, 1))).astype(np.float32),
        "pen": (np.random.uniform(1.0, 4.0, (N, 1))).astype(np.float32),
        "offs": striped(np.random.permutation(T)[:S]),
    }


def reference(x_words, x_scales, w1, w2, mult, budg, pen, offs):
    xq = unpack_weight(x_words, x_scales)[:, unstriped(offs)]
    yv = mxq(f64(w1), 0, "e4m3").T @ xq
    val = np.log(np.exp(yv) + 1.0) + 0.2
    bid = val / (np.repeat(f64(mult), D, axis=1) + 0.3)
    yp = mxq(f64(w2), 0, "e4m3").T @ xq
    pri = np.log(np.exp(yp) + 1.0)
    win = sigmoid(4.0 * (bid - pri))
    sur = win * (val - pri)
    pay = win * pri
    spend = pay.reshape(len(pay), -1, D).mean(axis=2)
    return sur.reshape(len(sur), -1, D).sum(axis=2) - (f64(pen) * (relu(spend - f64(budg)[:1])))

@@ -1,0 +1,166 @@
+from contextlib import ExitStack
+
+import concourse.mybir as mybir
+from concourse.masks import make_identity
+
+F32 = mybir.dt.float32
+BF16 = mybir.dt.bfloat16
+I32 = mybir.dt.int32
+U32 = mybir.dt.uint32
+U16 = mybir.dt.uint16
+U8 = mybir.dt.uint8
+FP8X4 = mybir.dt.float8_e4m3fn_x4
+ALU = mybir.AluOpType
+ACT = mybir.ActivationFunctionType
+
+P = 128
+K = 512
+T = 4096
+S = 1024
+D = 8
+N = 256
+V = 128
+HALF = S // 2
+VH = V // 2
+FLOOR = 2.0 ** -44
+
+FLOPS = 2 * K * 2 * N * S
+
+
+def tile_picked_ypacng_sur_p_kernel(tc, x_words, x_scales, w1, w2, mult, budg, pen, offs, out):
+    nc = tc.nc
+    with ExitStack() as ctx:
+        keep = ctx.enter_context(tc.tile_pool(name="keep", bufs=1))
+        psum = ctx.enter_context(tc.psum_pool(name="psum", bufs=1))
+
+        offsets = keep.tile([P, S // 16], U16, name="offsets")
+        nc.sync.dma_start(offsets[:], offs)
+
+        warm = keep.tile([P, 8], F32, name="warm")
+        warm_out = keep.tile([P, 8], F32, name="warm_out")
+        nc.gpsimd.memset(warm[:], 0.0)
+
+        xs = keep.tile([P, T], U8, name="xs", align_bytes=64)
+        for q in range(4):
+            nc.sync.dma_start(xs[32 * q : 32 * q + 32, :].bitcast(I32), x_scales[0, 4 * q : 4 * q + 4, :].bitcast(I32).partition_broadcast(8))
+        nc.scalar.activation(warm_out[:], warm[:], ACT.Sigmoid)
+
+        raw = [keep.tile([P, 4, N], F32, name="raw%d" % a) for a in range(2)]
+        xw = keep.tile([P, T], U32, name="xw", align_bytes=64)
+        nc.sync.dma_start(raw[0][:], w1.rearrange("(p j) n -> p j n", j=4))
+        nc.sync.dma_start(xw[:].bitcast(I32), x_words[0].rearrange("p n t -> p (n t)").bitcast(I32))
+        nc.sync.dma_start(raw[1][:], w2.rearrange("(p j) n -> p j n", j=4))
+        mul = keep.tile([P, 2, V], F32, name="mul")
+        nc.sync.dma_start(mul[:], mult.rearrange("(t p) v -> p t v", p=P))
+        bcol = keep.tile([P, 1], F32, name="bcol")
+        prow = keep.tile([P, N], F32, name="prow")
+        with nc.allow_non_contiguous_dma(reason="one value a partition"):
+            nc.sync.dma_start(bcol[:], budg[0:1, :].rearrange("o v -> v o"))
+        nc.sync.dma_start(prow[:], pen.rearrange("m o -> (m o)").partition_broadcast(P))
+
+        ident = keep.tile([P, P], F32, name="ident")
+        make_identity(nc, ident[:])
+
+        grouped = [keep.tile([P, N, 4], BF16, name="grouped%d" % a, align_bytes=64) for a in range(2)]
+        wq = [keep.tile([P, N], U32, name="wq%d" % a, align_bytes=64) for a in range(2)]
+        ws = [keep.tile([P, N], U8, name="ws%d" % a, align_bytes=64) for a in range(2)]
+
+        def quantise(a, ns):
+            nc.vector.quantize_mx(out=wq[a][:, ns].bitcast(FP8X4), scales=ws[a][:, ns], in_=grouped[a][:, ns, :].rearrange("p n j -> p (n j)"))
+
+        nc.scalar.copy(grouped[0][:], raw[0][:].rearrange("p j n -> p n j"))
+        xsg = keep.tile([P, S], U8, name="xsg", align_bytes=64)
+        nc.vector.tensor_copy(xsg[:], xs[:].indirect(offsets[:]))
+        quantise(0, slice(0, N))
+        xg = [keep.tile([P, HALF], U32, name="xg%d" % h, align_bytes=64) for h in range(2)]
+        for h in range(2):
+            nc.vector.tensor_copy(xg[h][:], xw[:].indirect(offsets[:, h * (HALF // 16) : (h + 1) * (HALF // 16)]))
+        for t in (1, 0):
+            ns = slice(t * P, (t + 1) * P)
+            nc.vector.tensor_copy(grouped[1][:, ns, :], raw[1][:, :, ns].rearrange("p j n -> p n j"))
+        for t in (1, 0):
+            quantise(1, slice(t * P, (t + 1) * P))
+        turned = psum.tile([P, 2, P], F32, name="turned", tag="b100")
+        for t in range(2):
+            nc.tensor.transpose(turned[:, t, :], mul[:, t, :], ident[:])
+        kn = keep.tile([P, 2, P], F32, name="kn")
+        nc.vector.tensor_scalar(kn[:], turned[:], 0.3, -0.5, ALU.add, ALU.mult)
+        mp = keep.tile([P, 2, V], F32, name="mp")
+        rp = keep.tile([P, 2, V], F32, name="rp")
+        b16 = keep.tile([P, 1], F32, name="b16")
+        nc.vector.tensor_scalar(mp[:], mul[:], 0.3, None, ALU.add)
+        nc.vector.tensor_scalar(b16[:], bcol[:], -16.0, None, ALU.mult)
+        nc.vector.reciprocal(rp[:], mp[:])
+
+        chunks = [(0, 0), (0, 1), (1, 0), (1, 1)]
+        y = {}
+        sig = {c: keep.tile([P, 2, D, VH], F32, name="sig%d%d" % c) for c in chunks}
+        order = [(0, 0, 0), (0, 1, 0), (0, 0, 1), (0, 1, 1), (1, 1, 1), (1, 1, 0), (1, 0, 1), (1, 0, 0)]
+        for a, t, h in order:
+            y[a, t, h] = psum.tile([P, HALF], F32, name="y%d%d%d" % (a, t, h), tag="b%d%d%d" % (a, t, h))
+            nc.tensor.matmul_mx(
+                out=y[a, t, h][:],
+                lhsT=wq[a][:, t * P : (t + 1) * P].bitcast(FP8X4),
+                lhsT_scale=ws[a][:, t * P : (t + 1) * P],
+                rhs=xg[h][:].bitcast(FP8X4),
+                rhs_scale=xsg[:, h * HALF : (h + 1) * HALF],
+                start=True,
+                stop=True,
+            )
+            nc.scalar.activation(sig[t, h][:, a, :, :], y[a, t, h][:].rearrange("p (v d) -> p d v", d=D), ACT.Sigmoid, scale=-1.0)
+
+        lg = {c: keep.tile([P, 2, D, VH], F32, name="lg%d%d" % c) for c in chunks}
+        pieces = {c: ([slice(0, 4), slice(4, 8)] if c == chunks[0] else [slice(0, 8)]) for c in chunks}
+        for c in chunks:
+            for ds in pieces[c]:
+                nc.scalar.activation(lg[c][:, :, ds, :], sig[c][:, :, ds, :], ACT.Ln, bias=FLOOR)
+
+        nv = {c: keep.tile([P, D, VH], F32, name="nv%d%d" % c) for c in chunks}
+        nb = {c: keep.tile([P, D, VH], F32, name="nb%d%d" % c) for c in chunks}
+        npr = [keep.tile([P, D, V], F32, name="npr%d" % t) for t in range(2)]
+        nu = [keep.tile([P, D, V], F32, name="nu%d" % t) for t in range(2)]
+        for i, c in enumerate(chunks):
+            t, h = c
+            vs = slice(h * VH, (h + 1) * VH)
+            for ds in pieces[c]:
+                yv = y[0, t, h][:].rearrange("p (v d) -> p d v", d=D)
+                yp = y[1, t, h][:].rearrange("p (v d) -> p d v", d=D)
+                nc.vector.scalar_tensor_tensor(nv[c][:, ds, :], yv[:, ds, :], -1.0, lg[c][:, 0, ds, :], ALU.mult, ALU.min)
+                nc.vector.scalar_tensor_tensor(npr[t][:, ds, vs], yp[:, ds, :], -1.0, lg[c][:, 1, ds, :], ALU.mult, ALU.min)
+            nc.vector.scalar_tensor_tensor(nb[c][:], nv[c][:], -0.2, rp[:, t : t + 1, vs].to_broadcast([P, D, VH]), ALU.add, ALU.mult)
+            eng = nc.gpsimd if i in [0,1,2] else nc.vector
+            eng.tensor_tensor(nu[t][:, :, vs], nb[c][:], npr[t][:, :, vs], ALU.subtract)
+
+        groups = [[[0,4],[4,8]],[[0,4],[4,6],[6,8]]]
+        acc_u = psum.tile([P, 2, P], F32, name="accu", tag="b000")
+        acc_p = psum.tile([P, 2, P], F32, name="accp", tag="b100")
+        for t in range(2):
+            su = keep.tile([P, D, V], F32, name="su%d" % t)
+            th = keep.tile([P, D, V], F32, name="th%d" % t)
+            pp = keep.tile([P, D, V], F32, name="pp%d" % t)
+            for d0, d1 in groups[t]:
+                ds = slice(d0, d1)
+                if t == 0 and d0 == 0:
+                    nc.scalar.activation(su[:, ds, :], nu[t][:, ds, :], ACT.Silu, scale=-4.0)
+                    nc.scalar.activation(th[:, ds, :], nu[t][:, ds, :], ACT.Tanh, scale=-2.0)
+                else:
+                    nc.scalar.activation(th[:, ds, :], nu[t][:, ds, :], ACT.Tanh, scale=-2.0)
+                    nc.scalar.activation(su[:, ds, :], nu[t][:, ds, :], ACT.Silu, scale=-4.0)
+                nc.vector.scalar_tensor_tensor(pp[:, ds, :], th[:, ds, :], 1.0, npr[t][:, ds, :], ALU.add, ALU.mult)
+                pairs = [(acc_u, su), (acc_p, pp)] if t == 0 else [(acc_p, pp), (acc_u, su)]
+                for acc, src in pairs:
+                    for d in range(d0, d1):
+                        nc.tensor.matmul(acc[:, t, :], src[:, d, :], ident[:], start=(d == 0), stop=(d == D - 1), is_transpose=True)
+        over = keep.tile([P, N], F32, name="over")
+        terms = [keep.tile([P, 2, P], F32, name="term%d" % i) for i in range(3)]
+        nc.scalar.activation(over[:], acc_p[:].rearrange("p t m -> p (t m)"), ACT.Relu, scale=-1.0, bias=b16[:, 0:1])
+        nc.vector.scalar_tensor_tensor(terms[0][:], kn[:], 0.5, acc_p[:], ALU.add, ALU.mult)
+        nc.vector.scalar_tensor_tensor(terms[1][:], acc_u[:], -0.5, kn[:], ALU.mult, ALU.mult)
+        nc.vector.scalar_tensor_tensor(terms[2][:].rearrange("p t m -> p (t m)"), over[:], -1.0 / 16.0, prow[:], ALU.mult, ALU.mult)
+        back = psum.tile([P, 2, P], F32, name="back", tag="b001")
+        for t in range(2):
+            for i in range(3):
+                nc.tensor.matmul(back[:, t, :], terms[i][:, t, :], ident[:], start=(i == 0), stop=(i == 2), is_transpose=True)
+        res = keep.tile([P, 2, V], F32, name="res")
+        nc.vector.tensor_copy(res[:], back[:])
+        nc.sync.dma_start(out.rearrange("(t p) v -> p t v", p=P), res[:])

@@ -38,25 +38,22 @@ def tile_picked_ypacng_sur_p_kernel(tc, x_words, x_scales, w1, w2, mult, budg, p
 
         warm = keep.tile([P, 8], F32, name="warm")
         warm_out = keep.tile([P, 8], F32, name="warm_out")
-        nc.gpsimd.memset(warm[:], 0.0)
 
-        xs = keep.tile([P, T], U8, name="xs", align_bytes=64)
-        for q in range(4):
-            nc.sync.dma_start(xs[32 * q : 32 * q + 32, :].bitcast(I32), x_scales[0, 4 * q : 4 * q + 4, :].bitcast(I32).partition_broadcast(8))
+        xs = keep.tile([P, T], U8, name="xs", tag="xs", align_bytes=64)
+        xsg = keep.tile([P, S], U8, name="xsg", align_bytes=64)
+        nc.vector.memset(xs[:].bitcast(I32), 0)
+        nc.vector.memset(warm[:], 0.0)
+        nc.vector.memset(xsg[:].bitcast(I32), 0)
+        nc.scalar.dma_start(xs[0:P:8, :].bitcast(I32), x_scales[0].bitcast(I32))
         nc.scalar.activation(warm_out[:], warm[:], ACT.Sigmoid)
 
-        raw = [keep.tile([P, 4, N], F32, name="raw%d" % a) for a in range(2)]
+        raw = [keep.tile([P, 4, N], F32, name="raw%d" % a, tag="raw%d" % a) for a in range(2)]
         xw = keep.tile([P, T], U32, name="xw", align_bytes=64)
         nc.sync.dma_start(raw[0][:], w1.rearrange("(p j) n -> p j n", j=4))
         nc.sync.dma_start(xw[:].bitcast(I32), x_words[0].rearrange("p n t -> p (n t)").bitcast(I32))
-        nc.sync.dma_start(raw[1][:], w2.rearrange("(p j) n -> p j n", j=4))
         mul = keep.tile([P, 2, V], F32, name="mul")
         nc.sync.dma_start(mul[:], mult.rearrange("(t p) v -> p t v", p=P))
-        bcol = keep.tile([P, 1], F32, name="bcol")
-        prow = keep.tile([P, N], F32, name="prow")
-        with nc.allow_non_contiguous_dma(reason="one value a partition"):
-            nc.sync.dma_start(bcol[:], budg[0:1, :].rearrange("o v -> v o"))
-        nc.sync.dma_start(prow[:], pen.rearrange("m o -> (m o)").partition_broadcast(P))
+        nc.sync.dma_start(raw[1][:], w2.rearrange("(p j) n -> p j n", j=4))
 
         ident = keep.tile([P, P], F32, name="ident")
         make_identity(nc, ident[:])
@@ -69,10 +66,12 @@ def tile_picked_ypacng_sur_p_kernel(tc, x_words, x_scales, w1, w2, mult, budg, p
             nc.vector.quantize_mx(out=wq[a][:, ns].bitcast(FP8X4), scales=ws[a][:, ns], in_=grouped[a][:, ns, :].rearrange("p n j -> p (n j)"))
 
         nc.scalar.copy(grouped[0][:], raw[0][:].rearrange("p j n -> p n j"))
-        xsg = keep.tile([P, S], U8, name="xsg", align_bytes=64)
-        nc.vector.tensor_copy(xsg[:], xs[:].indirect(offsets[:]))
+        spread = keep.tile([P, S], U8, name="spread", tag="spread", align_bytes=64)
+        nc.vector.tensor_copy(spread[:], xs[:].indirect(offsets[:]))
+        for q in range(4):
+            nc.sync.dma_start(xsg[32 * q : 32 * q + 4, :].bitcast(I32), spread[32 * q : 32 * q + 32 : 8, :].bitcast(I32))
         quantise(0, slice(0, N))
-        xg = [keep.tile([P, HALF], U32, name="xg%d" % h, align_bytes=64) for h in range(2)]
+        xg = [keep.tile([P, HALF], U32, name="xg%d" % h, tag=("xs" if h == 0 else "xg1"), align_bytes=64) for h in range(2)]
         for h in range(2):
             nc.vector.tensor_copy(xg[h][:], xw[:].indirect(offsets[:, h * (HALF // 16) : (h + 1) * (HALF // 16)]))
         for t in (1, 0):
@@ -80,6 +79,11 @@ def tile_picked_ypacng_sur_p_kernel(tc, x_words, x_scales, w1, w2, mult, budg, p
             nc.vector.tensor_copy(grouped[1][:, ns, :], raw[1][:, :, ns].rearrange("p j n -> p n j"))
         for t in (1, 0):
             quantise(1, slice(t * P, (t + 1) * P))
+        bcol = keep.tile([P, 1], F32, name="bcol", tag="raw1")
+        prow = keep.tile([P, N], F32, name="prow", tag="spread", align_bytes=64)
+        nc.sync.dma_start(prow[:], pen.rearrange("m o -> (m o)").partition_broadcast(P))
+        with nc.allow_non_contiguous_dma(reason="one value a partition"):
+            nc.sync.dma_start(bcol[:], budg[0:1, :].rearrange("o v -> v o"))
         turned = psum.tile([P, 2, P], F32, name="turned", tag="b100")
         for t in range(2):
             nc.tensor.transpose(turned[:, t, :], mul[:, t, :], ident[:])
@@ -89,8 +93,8 @@ def tile_picked_ypacng_sur_p_kernel(tc, x_words, x_scales, w1, w2, mult, budg, p
         rp = keep.tile([P, 2, V], F32, name="rp")
         b16 = keep.tile([P, 1], F32, name="b16")
         nc.vector.tensor_scalar(mp[:], mul[:], 0.3, None, ALU.add)
-        nc.vector.tensor_scalar(b16[:], bcol[:], -16.0, None, ALU.mult)
         nc.vector.reciprocal(rp[:], mp[:])
+        nc.vector.tensor_scalar(b16[:], bcol[:], -16.0, None, ALU.mult)
 
         chunks = [(0, 0), (0, 1), (1, 0), (1, 1)]
         y = {}
@@ -138,19 +142,26 @@ def tile_picked_ypacng_sur_p_kernel(tc, x_words, x_scales, w1, w2, mult, budg, p
             su = keep.tile([P, D, V], F32, name="su%d" % t)
             th = keep.tile([P, D, V], F32, name="th%d" % t)
             pp = keep.tile([P, D, V], F32, name="pp%d" % t)
-            for d0, d1 in groups[t]:
-                ds = slice(d0, d1)
-                if t == 0 and d0 == 0:
-                    nc.scalar.activation(su[:, ds, :], nu[t][:, ds, :], ACT.Silu, scale=-4.0)
-                    nc.scalar.activation(th[:, ds, :], nu[t][:, ds, :], ACT.Tanh, scale=-2.0)
-                else:
-                    nc.scalar.activation(th[:, ds, :], nu[t][:, ds, :], ACT.Tanh, scale=-2.0)
-                    nc.scalar.activation(su[:, ds, :], nu[t][:, ds, :], ACT.Silu, scale=-4.0)
-                nc.vector.scalar_tensor_tensor(pp[:, ds, :], th[:, ds, :], 1.0, npr[t][:, ds, :], ALU.add, ALU.mult)
-                pairs = [(acc_u, su), (acc_p, pp)] if t == 0 else [(acc_p, pp), (acc_u, su)]
-                for acc, src in pairs:
-                    for d in range(d0, d1):
-                        nc.tensor.matmul(acc[:, t, :], src[:, d, :], ident[:], start=(d == 0), stop=(d == D - 1), is_transpose=True)
+            def wins(ds, vs, silu_first):
+                funcs = [(su, ACT.Silu, -4.0), (th, ACT.Tanh, -2.0)]
+                for dst, func, scale in funcs if silu_first else reversed(funcs):
+                    nc.scalar.activation(dst[:, ds, vs], nu[t][:, ds, vs], func, scale=scale)
+                nc.vector.scalar_tensor_tensor(pp[:, ds, vs], th[:, ds, vs], 1.0, npr[t][:, ds, vs], ALU.add, ALU.mult)
+
+            def add_up(acc, src, d0, d1):
+                for d in range(d0, d1):
+                    nc.tensor.matmul(acc[:, t, :], src[:, d, :], ident[:], start=(d == 0), stop=(d == D - 1), is_transpose=True)
+
+            if t == 0:
+                for h in range(2):
+                    wins(slice(0, D), slice(h * VH, (h + 1) * VH), True)
+                add_up(acc_u, su, 0, D)
+                add_up(acc_p, pp, 0, D)
+            else:
+                for d0, d1 in groups[t]:
+                    wins(slice(d0, d1), slice(0, V), False)
+                    add_up(acc_p, pp, d0, d1)
+                    add_up(acc_u, su, d0, d1)
         over = keep.tile([P, N], F32, name="over")
         terms = [keep.tile([P, 2, P], F32, name="term%d" % i) for i in range(3)]
         nc.scalar.activation(over[:], acc_p[:].rearrange("p t m -> p (t m)"), ACT.Relu, scale=-1.0, bias=b16[:, 0:1])

@@ -69,7 +69,7 @@ def tile_picked_ypacng_sur_p_kernel(tc, x_words, x_scales, w1, w2, mult, budg, p
         spread = keep.tile([P, S], U8, name="spread", tag="spread", align_bytes=64)
         nc.vector.tensor_copy(spread[:], xs[:].indirect(offsets[:]))
         for q in range(4):
-            nc.sync.dma_start(xsg[32 * q : 32 * q + 4, :].bitcast(I32), spread[32 * q : 32 * q + 32 : 8, :].bitcast(I32))
+            nc.scalar.dma_start(xsg[32 * q : 32 * q + 4, :].bitcast(I32), spread[32 * q : 32 * q + 32 : 8, :].bitcast(I32))
         quantise(0, slice(0, N))
         xg = [keep.tile([P, HALF], U32, name="xg%d" % h, tag=("xs" if h == 0 else "xg1"), align_bytes=64) for h in range(2)]
         for h in range(2):
@@ -98,7 +98,7 @@ def tile_picked_ypacng_sur_p_kernel(tc, x_words, x_scales, w1, w2, mult, budg, p
 
         chunks = [(0, 0), (0, 1), (1, 0), (1, 1)]
         y = {}
-        sig = {c: keep.tile([P, 2, D, VH], F32, name="sig%d%d" % c) for c in chunks}
+        sig = {c: keep.tile([P, 2, HALF], F32, name="sig%d%d" % c) for c in chunks}
         order = [(0, 0, 0), (0, 1, 0), (0, 0, 1), (0, 1, 1), (1, 1, 1), (1, 1, 0), (1, 0, 1), (1, 0, 0)]
         for a, t, h in order:
             y[a, t, h] = psum.tile([P, HALF], F32, name="y%d%d%d" % (a, t, h), tag="b%d%d%d" % (a, t, h))
@@ -111,67 +111,106 @@ def tile_picked_ypacng_sur_p_kernel(tc, x_words, x_scales, w1, w2, mult, budg, p
                 start=True,
                 stop=True,
             )
-            nc.scalar.activation(sig[t, h][:, a, :, :], y[a, t, h][:].rearrange("p (v d) -> p d v", d=D), ACT.Sigmoid, scale=-1.0)
+            nc.scalar.activation(sig[t, h][:, a, :], y[a, t, h][:], ACT.Sigmoid, scale=-1.0)
 
-        lg = {c: keep.tile([P, 2, D, VH], F32, name="lg%d%d" % c) for c in chunks}
-        pieces = {c: ([slice(0, 4), slice(4, 8)] if c == chunks[0] else [slice(0, 8)]) for c in chunks}
+        lg = {c: keep.tile([P, 2, HALF], F32, name="lg%d%d" % c) for c in chunks}
+        pieces = {c: ([slice(0, HALF // 2), slice(HALF // 2, HALF)] if c == chunks[0] else [slice(0, HALF)]) for c in chunks}
         for c in chunks:
-            for ds in pieces[c]:
-                nc.scalar.activation(lg[c][:, :, ds, :], sig[c][:, :, ds, :], ACT.Ln, bias=FLOOR)
+            for js in pieces[c]:
+                nc.scalar.activation(lg[c][:, :, js], sig[c][:, :, js], ACT.Ln, bias=FLOOR)
 
-        nv = {c: keep.tile([P, D, VH], F32, name="nv%d%d" % c) for c in chunks}
-        nb = {c: keep.tile([P, D, VH], F32, name="nb%d%d" % c) for c in chunks}
-        npr = [keep.tile([P, D, V], F32, name="npr%d" % t) for t in range(2)]
-        nu = [keep.tile([P, D, V], F32, name="nu%d" % t) for t in range(2)]
-        for i, c in enumerate(chunks):
+        nv = {c: keep.tile([P, HALF], F32, name="nv%d%d" % c) for c in chunks}
+        nb = {c: keep.tile([P, HALF], F32, name="nb%d%d" % c) for c in chunks}
+        npr = [keep.tile([P, 2, HALF], F32, name="npr%d" % t) for t in range(2)]
+        nu = [keep.tile([P, 2, HALF], F32, name="nu%d" % t) for t in range(2)]
+
+        def soft(a, c, js):
             t, h = c
-            vs = slice(h * VH, (h + 1) * VH)
-            for ds in pieces[c]:
-                yv = y[0, t, h][:].rearrange("p (v d) -> p d v", d=D)
-                yp = y[1, t, h][:].rearrange("p (v d) -> p d v", d=D)
-                nc.vector.scalar_tensor_tensor(nv[c][:, ds, :], yv[:, ds, :], -1.0, lg[c][:, 0, ds, :], ALU.mult, ALU.min)
-                nc.vector.scalar_tensor_tensor(npr[t][:, ds, vs], yp[:, ds, :], -1.0, lg[c][:, 1, ds, :], ALU.mult, ALU.min)
-            nc.vector.scalar_tensor_tensor(nb[c][:], nv[c][:], -0.2, rp[:, t : t + 1, vs].to_broadcast([P, D, VH]), ALU.add, ALU.mult)
-            eng = nc.gpsimd if i in [0,1,2] else nc.vector
-            eng.tensor_tensor(nu[t][:, :, vs], nb[c][:], npr[t][:, :, vs], ALU.subtract)
+            dst = nv[c][:, js] if a == 0 else npr[t][:, h, js]
+            nc.vector.scalar_tensor_tensor(dst, y[a, t, h][:, js], -1.0, lg[c][:, a, js], ALU.mult, ALU.min)
 
-        groups = [[[0,4],[4,8]],[[0,4],[4,6],[6,8]]]
-        acc_u = psum.tile([P, 2, P], F32, name="accu", tag="b000")
-        acc_p = psum.tile([P, 2, P], F32, name="accp", tag="b100")
+        def bid(c):
+            t, h = c
+            nc.vector.scalar_tensor_tensor(
+                nb[c][:].rearrange("p (v d) -> p v d", d=D),
+                nv[c][:].rearrange("p (v d) -> p v d", d=D),
+                -0.2,
+                rp[:, t, h * VH : (h + 1) * VH].unsqueeze(2).to_broadcast([P, VH, D]),
+                ALU.add,
+                ALU.mult,
+            )
+
+        def gap(c, eng):
+            t, h = c
+            eng.tensor_tensor(nu[t][:, h, :], nb[c][:], npr[t][:, h, :], ALU.subtract)
+
+        whole = slice(0, HALF)
+        c0, c1, c2, c3 = chunks
+        for js in pieces[c0]:
+            soft(0, c0, js)
+            soft(1, c0, js)
+        bid(c0)
+        gap(c0, nc.gpsimd)
+        soft(0, c1, whole)
+        soft(1, c1, whole)
+        soft(0, c2, whole)
+        bid(c1)
+        gap(c1, nc.gpsimd)
+        soft(1, c2, whole)
+        soft(0, c3, whole)
+        soft(1, c3, whole)
+        bid(c2)
+        bid(c3)
+        gap(c2, nc.vector)
+        gap(c3, nc.vector)
+
+        acc_u = [psum.tile([P, P], F32, name="accu%d" % t, tag="b00%d" % t) for t in range(2)]
+        acc_p = [psum.tile([P, P], F32, name="accp%d" % t, tag="b10%d" % t) for t in range(2)]
         for t in range(2):
             su = keep.tile([P, D, V], F32, name="su%d" % t)
-            th = keep.tile([P, D, V], F32, name="th%d" % t)
+            th = keep.tile([P, D // 2, V, 2], F32, name="th%d" % t)
             pp = keep.tile([P, D, V], F32, name="pp%d" % t)
-            def wins(ds, vs, silu_first):
-                funcs = [(su, ACT.Silu, -4.0), (th, ACT.Tanh, -2.0)]
+            nu_pairs = nu[t][:].rearrange("p h (v g e) -> p g (h v) e", g=D // 2, e=2)
+            npr_pairs = npr[t][:].rearrange("p h (v g e) -> p g (h v) e", g=D // 2, e=2)
+            su_pairs = su[:].rearrange("p (g e) v -> p g v e", e=2)
+            pp_pairs = pp[:].rearrange("p (g e) v -> p g v e", e=2)
+
+            def wins(gs, vs, silu_first):
+                funcs = [(su_pairs, ACT.Silu, -4.0), (th, ACT.Tanh, -2.0)]
                 for dst, func, scale in funcs if silu_first else reversed(funcs):
-                    nc.scalar.activation(dst[:, ds, vs], nu[t][:, ds, vs], func, scale=scale)
-                nc.vector.scalar_tensor_tensor(pp[:, ds, vs], th[:, ds, vs], 1.0, npr[t][:, ds, vs], ALU.add, ALU.mult)
+                    nc.scalar.activation(dst[:, gs, vs, :], nu_pairs[:, gs, vs, :], func, scale=scale)
+
+            def pays(g):
+                nc.vector.scalar_tensor_tensor(pp_pairs[:, g, :, :], th[:, g, :, :], 1.0, npr_pairs[:, g, :, :], ALU.add, ALU.mult)
 
             def add_up(acc, src, d0, d1):
                 for d in range(d0, d1):
-                    nc.tensor.matmul(acc[:, t, :], src[:, d, :], ident[:], start=(d == 0), stop=(d == D - 1), is_transpose=True)
+                    nc.tensor.matmul(acc[t][:], src[:, d, :], ident[:], start=(d == 0), stop=(d == D - 1), is_transpose=True)
 
             if t == 0:
                 for h in range(2):
-                    wins(slice(0, D), slice(h * VH, (h + 1) * VH), True)
+                    wins(slice(0, D // 2), slice(h * VH, (h + 1) * VH), True)
                 add_up(acc_u, su, 0, D)
-                add_up(acc_p, pp, 0, D)
+                for g in range(D // 2):
+                    pays(g)
+                    add_up(acc_p, pp, 2 * g, 2 * g + 2)
             else:
-                for d0, d1 in groups[t]:
-                    wins(slice(d0, d1), slice(0, V), False)
-                    add_up(acc_p, pp, d0, d1)
-                    add_up(acc_u, su, d0, d1)
-        over = keep.tile([P, N], F32, name="over")
-        terms = [keep.tile([P, 2, P], F32, name="term%d" % i) for i in range(3)]
-        nc.scalar.activation(over[:], acc_p[:].rearrange("p t m -> p (t m)"), ACT.Relu, scale=-1.0, bias=b16[:, 0:1])
-        nc.vector.scalar_tensor_tensor(terms[0][:], kn[:], 0.5, acc_p[:], ALU.add, ALU.mult)
-        nc.vector.scalar_tensor_tensor(terms[1][:], acc_u[:], -0.5, kn[:], ALU.mult, ALU.mult)
-        nc.vector.scalar_tensor_tensor(terms[2][:].rearrange("p t m -> p (t m)"), over[:], -1.0 / 16.0, prow[:], ALU.mult, ALU.mult)
-        back = psum.tile([P, 2, P], F32, name="back", tag="b001")
+                for g0, g1 in [(0, 2), (2, 3), (3, 4)]:
+                    wins(slice(g0, g1), slice(0, V), False)
+                    for g in range(g0, g1):
+                        pays(g)
+                        add_up(acc_p, pp, 2 * g, 2 * g + 2)
+                    add_up(acc_u, su, 2 * g0, 2 * g1)
         for t in range(2):
+            over = keep.tile([P, P], F32, name="over%d" % t)
+            terms = [keep.tile([P, P], F32, name="term%d%d" % (t, i)) for i in range(3)]
+            nc.scalar.activation(over[:], acc_p[t][:], ACT.Relu, scale=-1.0, bias=b16[:, 0:1])
+            nc.vector.scalar_tensor_tensor(terms[0][:], acc_u[t][:], -0.5, kn[:, t, :], ALU.mult, ALU.mult)
+            nc.vector.scalar_tensor_tensor(terms[1][:], kn[:, t, :], 0.5, acc_p[t][:], ALU.add, ALU.mult)
+            nc.vector.scalar_tensor_tensor(terms[2][:], over[:], -1.0 / 16.0, prow[:, t * P : (t + 1) * P], ALU.mult, ALU.mult)
+            back = psum.tile([P, P], F32, name="back%d" % t, tag="b01%d" % t)
             for i in range(3):
-                nc.tensor.matmul(back[:, t, :], terms[i][:, t, :], ident[:], start=(i == 0), stop=(i == 2), is_transpose=True)
-        res = keep.tile([P, 2, V], F32, name="res")
-        nc.vector.tensor_copy(res[:], back[:])
-        nc.sync.dma_start(out.rearrange("(t p) v -> p t v", p=P), res[:])
+                nc.tensor.matmul(back[:], terms[i][:], ident[:], start=(i == 0), stop=(i == 2), is_transpose=True)
+            res = keep.tile([P, V], F32, name="res%d" % t)
+            nc.scalar.copy(res[:], back[:])
+            nc.sync.dma_start(out[t * P : (t + 1) * P, :], res[:])

@@ -31,6 +31,7 @@ def tile_picked_ypacng_sur_p_kernel(tc, x_words, x_scales, w1, w2, mult, budg, p
     nc = tc.nc
     with ExitStack() as ctx:
         keep = ctx.enter_context(tc.tile_pool(name="keep", bufs=1))
+        words = ctx.enter_context(tc.tile_pool(name="words", bufs=1))
         psum = ctx.enter_context(tc.psum_pool(name="psum", bufs=1))
 
         offsets = keep.tile([P, S // 16], U16, name="offsets")
@@ -39,57 +40,63 @@ def tile_picked_ypacng_sur_p_kernel(tc, x_words, x_scales, w1, w2, mult, budg, p
         warm = keep.tile([P, 8], F32, name="warm")
         warm_out = keep.tile([P, 8], F32, name="warm_out")
 
+        raw0 = keep.tile([P, 4, N], F32, name="raw0", tag="raw0")
+        nc.sync.dma_start(raw0[:], w1.rearrange("(p j) n -> p j n", j=4))
         xs = keep.tile([P, T], U8, name="xs", tag="xs", align_bytes=64)
         xsg = keep.tile([P, S], U8, name="xsg", align_bytes=64)
         nc.vector.memset(xs[:].bitcast(I32), 0)
-        nc.vector.memset(warm[:], 0.0)
-        nc.vector.memset(xsg[:].bitcast(I32), 0)
-        nc.scalar.dma_start(xs[0:P:8, :].bitcast(I32), x_scales[0].bitcast(I32))
-        nc.scalar.activation(warm_out[:], warm[:], ACT.Sigmoid)
-
-        raw = [keep.tile([P, 4, N], F32, name="raw%d" % a, tag="raw%d" % a) for a in range(2)]
-        xw = keep.tile([P, T], U32, name="xw", align_bytes=64)
-        nc.sync.dma_start(raw[0][:], w1.rearrange("(p j) n -> p j n", j=4))
-        nc.sync.dma_start(xw[:].bitcast(I32), x_words[0].rearrange("p n t -> p (n t)").bitcast(I32))
-        mul = keep.tile([P, 2, V], F32, name="mul")
-        nc.sync.dma_start(mul[:], mult.rearrange("(t p) v -> p t v", p=P))
-        nc.sync.dma_start(raw[1][:], w2.rearrange("(p j) n -> p j n", j=4))
-
+        nc.sync.dma_start(xs[0:P:8, :].bitcast(I32), x_scales[0].bitcast(I32))
+        one = words.tile([P, 1], F32, name="one", offset=0, align_bytes=64)
+        floor = keep.tile([P, 1], F32, name="floor")
+        nc.vector.memset(one[:], 1.0)
+        nc.vector.tensor_scalar(floor[:], one[:], FLOOR, None, ALU.mult)
         ident = keep.tile([P, P], F32, name="ident")
         make_identity(nc, ident[:])
+        nc.vector.memset(xsg[:].bitcast(I32), 0)
+        nc.gpsimd.memset(warm[:], 0.0)
+        nc.scalar.activation(warm_out[:], warm[:], ACT.Sigmoid)
+        xw = words.tile([P, T], U32, name="xw", offset=0, align_bytes=64)
+        nc.sync.dma_start(xw[:].bitcast(I32), x_words[0].rearrange("p n t -> p (n t)").bitcast(I32))
 
-        grouped = [keep.tile([P, N, 4], BF16, name="grouped%d" % a, align_bytes=64) for a in range(2)]
+        grouped = [
+            keep.tile([P, N, 4], BF16, name="grouped0", align_bytes=64),
+            words.tile([P, N, 4], BF16, name="grouped1", offset=0, align_bytes=64),
+        ]
         wq = [keep.tile([P, N], U32, name="wq%d" % a, align_bytes=64) for a in range(2)]
         ws = [keep.tile([P, N], U8, name="ws%d" % a, align_bytes=64) for a in range(2)]
 
         def quantise(a, ns):
             nc.vector.quantize_mx(out=wq[a][:, ns].bitcast(FP8X4), scales=ws[a][:, ns], in_=grouped[a][:, ns, :].rearrange("p n j -> p (n j)"))
 
-        nc.scalar.copy(grouped[0][:], raw[0][:].rearrange("p j n -> p n j"))
+        nc.scalar.copy(grouped[0][:], raw0[:].rearrange("p j n -> p n j"))
+        mul = keep.tile([P, 2, V], F32, name="mul", tag="raw0")
+        nc.sync.dma_start(mul[:], mult.rearrange("(t p) v -> p t v", p=P))
         spread = keep.tile([P, S], U8, name="spread", tag="spread", align_bytes=64)
         nc.vector.tensor_copy(spread[:], xs[:].indirect(offsets[:]))
         for q in range(4):
-            nc.scalar.dma_start(xsg[32 * q : 32 * q + 4, :].bitcast(I32), spread[32 * q : 32 * q + 32 : 8, :].bitcast(I32))
+            nc.sync.dma_start(xsg[32 * q : 32 * q + 4, :].bitcast(I32), spread[32 * q : 32 * q + 32 : 8, :].bitcast(I32))
+        raw1 = keep.tile([P, 4, N], F32, name="raw1", tag="xs", align_bytes=64)
+        nc.sync.dma_start(raw1[:], w2.rearrange("(p j) n -> p j n", j=4))
         quantise(0, slice(0, N))
-        xg = [keep.tile([P, HALF], U32, name="xg%d" % h, tag=("xs" if h == 0 else "xg1"), align_bytes=64) for h in range(2)]
+        xg = [keep.tile([P, HALF], U32, name="xg%d" % h, align_bytes=64) for h in range(2)]
         for h in range(2):
             nc.vector.tensor_copy(xg[h][:], xw[:].indirect(offsets[:, h * (HALF // 16) : (h + 1) * (HALF // 16)]))
         for t in (1, 0):
             ns = slice(t * P, (t + 1) * P)
-            nc.vector.tensor_copy(grouped[1][:, ns, :], raw[1][:, :, ns].rearrange("p j n -> p n j"))
+            nc.vector.tensor_copy(grouped[1][:, ns, :], raw1[:, :, ns].rearrange("p j n -> p n j"))
         for t in (1, 0):
             quantise(1, slice(t * P, (t + 1) * P))
-        bcol = keep.tile([P, 1], F32, name="bcol", tag="raw1")
-        prow = keep.tile([P, N], F32, name="prow", tag="spread", align_bytes=64)
+        bcol = words.tile([P, 1], F32, name="bcol", offset=5120, align_bytes=64)
+        prow = words.tile([P, N], F32, name="prow", offset=4096, align_bytes=64)
         nc.sync.dma_start(prow[:], pen.rearrange("m o -> (m o)").partition_broadcast(P))
         with nc.allow_non_contiguous_dma(reason="one value a partition"):
             nc.sync.dma_start(bcol[:], budg[0:1, :].rearrange("o v -> v o"))
         turned = psum.tile([P, 2, P], F32, name="turned", tag="b100")
         for t in range(2):
             nc.tensor.transpose(turned[:, t, :], mul[:, t, :], ident[:])
-        kn = keep.tile([P, 2, P], F32, name="kn")
+        kn = words.tile([P, 2, P], F32, name="kn", offset=2048, align_bytes=64)
         nc.vector.tensor_scalar(kn[:], turned[:], 0.3, -0.5, ALU.add, ALU.mult)
-        mp = keep.tile([P, 2, V], F32, name="mp")
+        mp = words.tile([P, 2, V], F32, name="mp", offset=0, align_bytes=64)
         rp = keep.tile([P, 2, V], F32, name="rp")
         b16 = keep.tile([P, 1], F32, name="b16")
         nc.vector.tensor_scalar(mp[:], mul[:], 0.3, None, ALU.add)
@@ -117,7 +124,7 @@ def tile_picked_ypacng_sur_p_kernel(tc, x_words, x_scales, w1, w2, mult, budg, p
         pieces = {c: ([slice(0, HALF // 2), slice(HALF // 2, HALF)] if c == chunks[0] else [slice(0, HALF)]) for c in chunks}
         for c in chunks:
             for js in pieces[c]:
-                nc.scalar.activation(lg[c][:, :, js], sig[c][:, :, js], ACT.Ln, bias=FLOOR)
+                nc.scalar.activation(lg[c][:, :, js], sig[c][:, :, js], ACT.Ln, bias=floor[:, 0:1])
 
         nv = {c: keep.tile([P, HALF], F32, name="nv%d%d" % c) for c in chunks}
         nb = {c: keep.tile([P, HALF], F32, name="nb%d%d" % c) for c in chunks}

@@ -15,6 +15,7 @@ ACT = mybir.ActivationFunctionType
 
 P = 128
 K = 512
+PACK = 4
 T = 4096
 S = 1024
 D = 8
@@ -22,7 +23,9 @@ N = 256
 V = 128
 HALF = S // 2
 VH = V // 2
-FLOOR = 2.0 ** -44
+PAIRS = D // 2
+CAP = 30.0
+VALUE, PRICE = 0, 1
 
 FLOPS = 2 * K * 2 * N * S
 
@@ -31,193 +34,211 @@ def tile_picked_ypacng_sur_p_kernel(tc, x_words, x_scales, w1, w2, mult, budg, p
     nc = tc.nc
     with ExitStack() as ctx:
         keep = ctx.enter_context(tc.tile_pool(name="keep", bufs=1))
-        words = ctx.enter_context(tc.tile_pool(name="words", bufs=1))
+        shared = ctx.enter_context(tc.tile_pool(name="shared", bufs=1))
         psum = ctx.enter_context(tc.psum_pool(name="psum", bufs=1))
 
         offsets = keep.tile([P, S // 16], U16, name="offsets")
         nc.sync.dma_start(offsets[:], offs)
 
-        warm = keep.tile([P, 8], F32, name="warm")
-        warm_out = keep.tile([P, 8], F32, name="warm_out")
+        raw_value = keep.tile([P, PACK, N], F32, name="raw_value", tag="raw_value")
+        nc.sync.dma_start(raw_value[:], w1.rearrange("(p j) n -> p j n", j=PACK))
 
-        raw0 = keep.tile([P, 4, N], F32, name="raw0", tag="raw0")
-        nc.sync.dma_start(raw0[:], w1.rearrange("(p j) n -> p j n", j=4))
-        xs = keep.tile([P, T], U8, name="xs", tag="xs", align_bytes=64)
-        xsg = keep.tile([P, S], U8, name="xsg", align_bytes=64)
-        nc.vector.memset(xs[:].bitcast(I32), 0)
-        nc.sync.dma_start(xs[0:P:8, :].bitcast(I32), x_scales[0].bitcast(I32))
-        one = words.tile([P, 1], F32, name="one", offset=0, align_bytes=64)
+        scale_table = keep.tile([P, T], U8, name="scale_table", tag="scale_table", align_bytes=64)
+        x_scale = keep.tile([P, S], U8, name="x_scale", align_bytes=64)
+        nc.vector.memset(scale_table[:].bitcast(I32), 0)
+        nc.sync.dma_start(scale_table[0:P:8, :].bitcast(I32), x_scales[0].bitcast(I32))
+
+        one = shared.tile([P, 1], F32, name="one", offset=0, align_bytes=64)
         floor = keep.tile([P, 1], F32, name="floor")
         nc.vector.memset(one[:], 1.0)
-        nc.vector.tensor_scalar(floor[:], one[:], FLOOR, None, ALU.mult)
+        cap = keep.tile([P, 1], F32, name="cap")
+        nc.vector.tensor_scalar(cap[:], one[:], CAP, None, ALU.mult)
+        nc.scalar.activation(floor[:], cap[:], ACT.Sigmoid, scale=-1.0)
         ident = keep.tile([P, P], F32, name="ident")
         make_identity(nc, ident[:])
-        nc.vector.memset(xsg[:].bitcast(I32), 0)
-        nc.gpsimd.memset(warm[:], 0.0)
-        nc.scalar.activation(warm_out[:], warm[:], ACT.Sigmoid)
-        xw = words.tile([P, T], U32, name="xw", offset=0, align_bytes=64)
-        nc.sync.dma_start(xw[:].bitcast(I32), x_words[0].rearrange("p n t -> p (n t)").bitcast(I32))
+        nc.vector.memset(x_scale[:].bitcast(I32), 0)
+        word_table = shared.tile([P, T], U32, name="word_table", offset=0, align_bytes=64)
+        nc.sync.dma_start(word_table[:].bitcast(I32), x_words[0].rearrange("p n t -> p (n t)").bitcast(I32))
 
         grouped = [
-            keep.tile([P, N, 4], BF16, name="grouped0", align_bytes=64),
-            words.tile([P, N, 4], BF16, name="grouped1", offset=0, align_bytes=64),
+            keep.tile([P, N, PACK], BF16, name="grouped_value", align_bytes=64),
+            shared.tile([P, N, PACK], BF16, name="grouped_price", offset=0, align_bytes=64),
         ]
-        wq = [keep.tile([P, N], U32, name="wq%d" % a, align_bytes=64) for a in range(2)]
-        ws = [keep.tile([P, N], U8, name="ws%d" % a, align_bytes=64) for a in range(2)]
+        w_word = [keep.tile([P, N], U32, name="w_word%d" % a, align_bytes=64) for a in (VALUE, PRICE)]
+        w_scale = [keep.tile([P, N], U8, name="w_scale%d" % a, align_bytes=64) for a in (VALUE, PRICE)]
 
-        def quantise(a, ns):
-            nc.vector.quantize_mx(out=wq[a][:, ns].bitcast(FP8X4), scales=ws[a][:, ns], in_=grouped[a][:, ns, :].rearrange("p n j -> p (n j)"))
+        def quantise(a, cols):
+            nc.vector.quantize_mx(
+                out=w_word[a][:, cols].bitcast(FP8X4),
+                scales=w_scale[a][:, cols],
+                in_=grouped[a][:, cols, :].rearrange("p n j -> p (n j)"),
+            )
 
-        nc.scalar.copy(grouped[0][:], raw0[:].rearrange("p j n -> p n j"))
-        mul = keep.tile([P, 2, V], F32, name="mul", tag="raw0")
-        nc.sync.dma_start(mul[:], mult.rearrange("(t p) v -> p t v", p=P))
-        spread = keep.tile([P, S], U8, name="spread", tag="spread", align_bytes=64)
-        nc.vector.tensor_copy(spread[:], xs[:].indirect(offsets[:]))
+        nc.scalar.copy(grouped[VALUE][:], raw_value[:].rearrange("p j n -> p n j"))
+        mult_rows = keep.tile([P, 2, V], F32, name="mult_rows", tag="raw_value")
+        nc.sync.dma_start(mult_rows[:], mult.rearrange("(t p) v -> p t v", p=P))
+
+        picked_scale = keep.tile([P, S], U8, name="picked_scale", align_bytes=64)
+        nc.vector.tensor_copy(picked_scale[:], scale_table[:].indirect(offsets[:]))
         for q in range(4):
-            nc.sync.dma_start(xsg[32 * q : 32 * q + 4, :].bitcast(I32), spread[32 * q : 32 * q + 32 : 8, :].bitcast(I32))
-        raw1 = keep.tile([P, 4, N], F32, name="raw1", tag="xs", align_bytes=64)
-        nc.sync.dma_start(raw1[:], w2.rearrange("(p j) n -> p j n", j=4))
-        quantise(0, slice(0, N))
-        xg = [keep.tile([P, HALF], U32, name="xg%d" % h, align_bytes=64) for h in range(2)]
-        for h in range(2):
-            nc.vector.tensor_copy(xg[h][:], xw[:].indirect(offsets[:, h * (HALF // 16) : (h + 1) * (HALF // 16)]))
-        for t in (1, 0):
-            ns = slice(t * P, (t + 1) * P)
-            nc.vector.tensor_copy(grouped[1][:, ns, :], raw1[:, :, ns].rearrange("p j n -> p n j"))
-        for t in (1, 0):
-            quantise(1, slice(t * P, (t + 1) * P))
-        bcol = words.tile([P, 1], F32, name="bcol", offset=5120, align_bytes=64)
-        prow = words.tile([P, N], F32, name="prow", offset=4096, align_bytes=64)
-        nc.sync.dma_start(prow[:], pen.rearrange("m o -> (m o)").partition_broadcast(P))
-        with nc.allow_non_contiguous_dma(reason="one value a partition"):
-            nc.sync.dma_start(bcol[:], budg[0:1, :].rearrange("o v -> v o"))
-        turned = psum.tile([P, 2, P], F32, name="turned", tag="b100")
-        for t in range(2):
-            nc.tensor.transpose(turned[:, t, :], mul[:, t, :], ident[:])
-        kn = words.tile([P, 2, P], F32, name="kn", offset=2048, align_bytes=64)
-        nc.vector.tensor_scalar(kn[:], turned[:], 0.3, -0.5, ALU.add, ALU.mult)
-        mp = words.tile([P, 2, V], F32, name="mp", offset=0, align_bytes=64)
-        rp = keep.tile([P, 2, V], F32, name="rp")
-        b16 = keep.tile([P, 1], F32, name="b16")
-        nc.vector.tensor_scalar(mp[:], mul[:], 0.3, None, ALU.add)
-        nc.vector.reciprocal(rp[:], mp[:])
-        nc.vector.tensor_scalar(b16[:], bcol[:], -16.0, None, ALU.mult)
+            nc.sync.dma_start(x_scale[32 * q : 32 * q + 4, :].bitcast(I32), picked_scale[32 * q : 32 * q + 32 : 8, :].bitcast(I32))
+        raw_price = keep.tile([P, PACK, N], F32, name="raw_price", tag="scale_table", align_bytes=64)
+        nc.sync.dma_start(raw_price[:], w2.rearrange("(p j) n -> p j n", j=PACK))
+        quantise(VALUE, slice(0, N))
 
-        chunks = [(0, 0), (0, 1), (1, 0), (1, 1)]
+        x_word = [keep.tile([P, HALF], U32, name="x_word%d" % h, align_bytes=64) for h in range(2)]
+        for h in range(2):
+            nc.vector.tensor_copy(x_word[h][:], word_table[:].indirect(offsets[:, h * (HALF // 16) : (h + 1) * (HALF // 16)]))
+
+        for t in (1, 0):
+            cols = slice(t * P, (t + 1) * P)
+            nc.vector.tensor_copy(grouped[PRICE][:, cols, :], raw_price[:, :, cols].rearrange("p j n -> p n j"))
+        for t in (1, 0):
+            quantise(PRICE, slice(t * P, (t + 1) * P))
+
+        budg_col = shared.tile([P, 1], F32, name="budg_col", offset=5120, align_bytes=64)
+        pen_row = shared.tile([P, N], F32, name="pen_row", offset=4096, align_bytes=64)
+        nc.sync.dma_start(pen_row[:], pen.rearrange("m o -> (m o)").partition_broadcast(P))
+        with nc.allow_non_contiguous_dma(reason="one value a partition"):
+            nc.sync.dma_start(budg_col[:], budg[0:1, :].rearrange("o v -> v o"))
+
+        def bank(a, t, h):
+            return "bank%d%d%d" % (a, t, h)
+
+        mult_turned = psum.tile([P, 2, P], F32, name="mult_turned", tag=bank(PRICE, 0, 0))
+        for t in range(2):
+            nc.tensor.transpose(mult_turned[:, t, :], mult_rows[:, t, :], ident[:])
+        neg_half_m = shared.tile([P, 2, P], F32, name="neg_half_m", offset=1024, align_bytes=64)
+        nc.vector.tensor_scalar(neg_half_m[:], mult_turned[:], 0.3, -0.5, ALU.add, ALU.mult)
+        m_rows = shared.tile([P, 2, V], F32, name="m_rows", offset=0, align_bytes=64)
+        inv_m = keep.tile([P, 2, V], F32, name="inv_m")
+        neg_budg16 = shared.tile([P, 1], F32, name="neg_budg16", offset=6144, align_bytes=64)
+        nc.vector.tensor_scalar(m_rows[:], mult_rows[:], 0.3, None, ALU.add)
+        nc.vector.reciprocal(inv_m[:], m_rows[:])
+        nc.vector.tensor_scalar(neg_budg16[:], budg_col[:], -16.0, None, ALU.mult)
+
+        chunks = [(t, h) for t in range(2) for h in range(2)]
+        products = [(VALUE, t, h) for h in range(2) for t in range(2)] + [(PRICE, t, h) for t, h in reversed(chunks)]
         y = {}
         sig = {c: keep.tile([P, 2, HALF], F32, name="sig%d%d" % c) for c in chunks}
-        order = [(0, 0, 0), (0, 1, 0), (0, 0, 1), (0, 1, 1), (1, 1, 1), (1, 1, 0), (1, 0, 1), (1, 0, 0)]
-        for a, t, h in order:
-            y[a, t, h] = psum.tile([P, HALF], F32, name="y%d%d%d" % (a, t, h), tag="b%d%d%d" % (a, t, h))
+        for a, t, h in products:
+            y[a, t, h] = psum.tile([P, HALF], F32, name="y%d%d%d" % (a, t, h), tag=bank(a, t, h))
             nc.tensor.matmul_mx(
                 out=y[a, t, h][:],
-                lhsT=wq[a][:, t * P : (t + 1) * P].bitcast(FP8X4),
-                lhsT_scale=ws[a][:, t * P : (t + 1) * P],
-                rhs=xg[h][:].bitcast(FP8X4),
-                rhs_scale=xsg[:, h * HALF : (h + 1) * HALF],
+                lhsT=w_word[a][:, t * P : (t + 1) * P].bitcast(FP8X4),
+                lhsT_scale=w_scale[a][:, t * P : (t + 1) * P],
+                rhs=x_word[h][:].bitcast(FP8X4),
+                rhs_scale=x_scale[:, h * HALF : (h + 1) * HALF],
                 start=True,
                 stop=True,
             )
             nc.scalar.activation(sig[t, h][:, a, :], y[a, t, h][:], ACT.Sigmoid, scale=-1.0)
 
-        lg = {c: keep.tile([P, 2, HALF], F32, name="lg%d%d" % c) for c in chunks}
-        pieces = {c: ([slice(0, HALF // 2), slice(HALF // 2, HALF)] if c == chunks[0] else [slice(0, HALF)]) for c in chunks}
+        whole = slice(0, HALF)
+        first_pieces = [slice(0, HALF // 2), slice(HALF // 2, HALF)]
+        log_sig = {c: keep.tile([P, 2, HALF], F32, name="log_sig%d%d" % c) for c in chunks}
         for c in chunks:
-            for js in pieces[c]:
-                nc.scalar.activation(lg[c][:, :, js], sig[c][:, :, js], ACT.Ln, bias=floor[:, 0:1])
+            for js in first_pieces if c == chunks[0] else [whole]:
+                nc.scalar.activation(log_sig[c][:, :, js], sig[c][:, :, js], ACT.Ln, bias=floor[:, 0:1])
 
-        nv = {c: keep.tile([P, HALF], F32, name="nv%d%d" % c) for c in chunks}
-        nb = {c: keep.tile([P, HALF], F32, name="nb%d%d" % c) for c in chunks}
-        npr = [keep.tile([P, 2, HALF], F32, name="npr%d" % t) for t in range(2)]
-        nu = [keep.tile([P, 2, HALF], F32, name="nu%d" % t) for t in range(2)]
+        neg_soft = {c: keep.tile([P, HALF], F32, name="neg_soft%d%d" % c) for c in chunks}
+        neg_bid = {c: keep.tile([P, HALF], F32, name="neg_bid%d%d" % c) for c in chunks}
+        neg_pri = [keep.tile([P, 2, HALF], F32, name="neg_pri%d" % t) for t in range(2)]
+        neg_u = [keep.tile([P, 2, HALF], F32, name="neg_u%d" % t) for t in range(2)]
 
-        def soft(a, c, js):
+        def softplus(a, c, js):
             t, h = c
-            dst = nv[c][:, js] if a == 0 else npr[t][:, h, js]
-            nc.vector.scalar_tensor_tensor(dst, y[a, t, h][:, js], -1.0, lg[c][:, a, js], ALU.mult, ALU.min)
+            dst = neg_soft[c][:, js] if a == VALUE else neg_pri[t][:, h, js]
+            nc.vector.scalar_tensor_tensor(dst, y[a, t, h][:, js], -1.0, log_sig[c][:, a, js], ALU.mult, ALU.min)
 
         def bid(c):
             t, h = c
             nc.vector.scalar_tensor_tensor(
-                nb[c][:].rearrange("p (v d) -> p v d", d=D),
-                nv[c][:].rearrange("p (v d) -> p v d", d=D),
+                neg_bid[c][:].rearrange("p (v d) -> p v d", d=D),
+                neg_soft[c][:].rearrange("p (v d) -> p v d", d=D),
                 -0.2,
-                rp[:, t, h * VH : (h + 1) * VH].unsqueeze(2).to_broadcast([P, VH, D]),
+                inv_m[:, t, h * VH : (h + 1) * VH].unsqueeze(2).to_broadcast([P, VH, D]),
                 ALU.add,
                 ALU.mult,
             )
 
-        def gap(c, eng):
+        def margin(c, engine):
             t, h = c
-            eng.tensor_tensor(nu[t][:, h, :], nb[c][:], npr[t][:, h, :], ALU.subtract)
+            engine.tensor_tensor(neg_u[t][:, h, :], neg_bid[c][:], neg_pri[t][:, h, :], ALU.subtract)
 
-        whole = slice(0, HALF)
         c0, c1, c2, c3 = chunks
-        for js in pieces[c0]:
-            soft(0, c0, js)
-            soft(1, c0, js)
+        for js in first_pieces:
+            softplus(VALUE, c0, js)
+            softplus(PRICE, c0, js)
         bid(c0)
-        gap(c0, nc.gpsimd)
-        soft(0, c1, whole)
-        soft(1, c1, whole)
-        soft(0, c2, whole)
+        margin(c0, nc.gpsimd)
+        softplus(VALUE, c1, whole)
+        softplus(PRICE, c1, whole)
+        softplus(VALUE, c2, whole)
         bid(c1)
-        gap(c1, nc.gpsimd)
-        soft(1, c2, whole)
-        soft(0, c3, whole)
-        soft(1, c3, whole)
+        margin(c1, nc.gpsimd)
+        softplus(PRICE, c2, whole)
+        softplus(VALUE, c3, whole)
+        softplus(PRICE, c3, whole)
         bid(c2)
         bid(c3)
-        gap(c2, nc.vector)
-        gap(c3, nc.vector)
+        margin(c2, nc.vector)
+        margin(c3, nc.vector)
 
-        acc_u = [psum.tile([P, P], F32, name="accu%d" % t, tag="b00%d" % t) for t in range(2)]
-        acc_p = [psum.tile([P, P], F32, name="accp%d" % t, tag="b10%d" % t) for t in range(2)]
+        sum_u = [psum.tile([P, P], F32, name="sum_u%d" % t, tag=bank(VALUE, 0, t)) for t in range(2)]
+        sum_r = [psum.tile([P, P], F32, name="sum_r%d" % t, tag=bank(PRICE, 0, t)) for t in range(2)]
         for t in range(2):
-            su = keep.tile([P, D, V], F32, name="su%d" % t)
-            th = keep.tile([P, D // 2, V, 2], F32, name="th%d" % t)
-            pp = keep.tile([P, D, V], F32, name="pp%d" % t)
-            nu_pairs = nu[t][:].rearrange("p h (v g e) -> p g (h v) e", g=D // 2, e=2)
-            npr_pairs = npr[t][:].rearrange("p h (v g e) -> p g (h v) e", g=D // 2, e=2)
-            su_pairs = su[:].rearrange("p (g e) v -> p g v e", e=2)
-            pp_pairs = pp[:].rearrange("p (g e) v -> p g v e", e=2)
+            u_terms = keep.tile([P, D, V], F32, name="u_terms%d" % t)
+            tanh_u = keep.tile([P, PAIRS, V, 2], F32, name="tanh_u%d" % t)
+            r_terms = keep.tile([P, D, V], F32, name="r_terms%d" % t)
+            neg_u_pairs = neg_u[t][:].rearrange("p h (v g e) -> p g (h v) e", g=PAIRS, e=2)
+            neg_pri_pairs = neg_pri[t][:].rearrange("p h (v g e) -> p g (h v) e", g=PAIRS, e=2)
+            u_terms_pairs = u_terms[:].rearrange("p (g e) v -> p g v e", e=2)
+            r_terms_pairs = r_terms[:].rearrange("p (g e) v -> p g v e", e=2)
 
-            def wins(gs, vs, silu_first):
-                funcs = [(su_pairs, ACT.Silu, -4.0), (th, ACT.Tanh, -2.0)]
-                for dst, func, scale in funcs if silu_first else reversed(funcs):
-                    nc.scalar.activation(dst[:, gs, vs, :], nu_pairs[:, gs, vs, :], func, scale=scale)
+            def silu(gs, vs):
+                nc.scalar.activation(u_terms_pairs[:, gs, vs, :], neg_u_pairs[:, gs, vs, :], ACT.Silu, scale=-4.0)
 
-            def pays(g):
-                nc.vector.scalar_tensor_tensor(pp_pairs[:, g, :, :], th[:, g, :, :], 1.0, npr_pairs[:, g, :, :], ALU.add, ALU.mult)
+            def tanh(gs, vs):
+                nc.scalar.activation(tanh_u[:, gs, vs, :], neg_u_pairs[:, gs, vs, :], ACT.Tanh, scale=-2.0)
 
-            def add_up(acc, src, d0, d1):
+            def add_up(acc, terms, d0, d1):
                 for d in range(d0, d1):
-                    nc.tensor.matmul(acc[t][:], src[:, d, :], ident[:], start=(d == 0), stop=(d == D - 1), is_transpose=True)
+                    nc.tensor.matmul(acc[:], terms[:, d, :], ident[:], start=(d == 0), stop=(d == D - 1), is_transpose=True)
 
+            def payments(g):
+                nc.vector.scalar_tensor_tensor(r_terms_pairs[:, g, :, :], tanh_u[:, g, :, :], 1.0, neg_pri_pairs[:, g, :, :], ALU.add, ALU.mult)
+                add_up(sum_r[t], r_terms, 2 * g, 2 * g + 2)
+
+            every_pair = slice(0, PAIRS)
             if t == 0:
                 for h in range(2):
-                    wins(slice(0, D // 2), slice(h * VH, (h + 1) * VH), True)
-                add_up(acc_u, su, 0, D)
-                for g in range(D // 2):
-                    pays(g)
-                    add_up(acc_p, pp, 2 * g, 2 * g + 2)
+                    silu(every_pair, slice(h * VH, (h + 1) * VH))
+                    tanh(every_pair, slice(h * VH, (h + 1) * VH))
+                add_up(sum_u[t], u_terms, 0, D)
+                for g in range(PAIRS):
+                    payments(g)
             else:
+                tanh(every_pair, slice(0, VH))
+                silu(every_pair, slice(0, VH))
                 for g0, g1 in [(0, 2), (2, 3), (3, 4)]:
-                    wins(slice(g0, g1), slice(0, V), False)
+                    tanh(slice(g0, g1), slice(VH, V))
+                    silu(slice(g0, g1), slice(VH, V))
                     for g in range(g0, g1):
-                        pays(g)
-                        add_up(acc_p, pp, 2 * g, 2 * g + 2)
-                    add_up(acc_u, su, 2 * g0, 2 * g1)
+                        payments(g)
+                    add_up(sum_u[t], u_terms, 2 * g0, 2 * g1)
+
+        over = [keep.tile([P, P], F32, name="over%d" % t) for t in range(2)]
         for t in range(2):
-            over = keep.tile([P, P], F32, name="over%d" % t)
-            terms = [keep.tile([P, P], F32, name="term%d%d" % (t, i)) for i in range(3)]
-            nc.scalar.activation(over[:], acc_p[t][:], ACT.Relu, scale=-1.0, bias=b16[:, 0:1])
-            nc.vector.scalar_tensor_tensor(terms[0][:], acc_u[t][:], -0.5, kn[:, t, :], ALU.mult, ALU.mult)
-            nc.vector.scalar_tensor_tensor(terms[1][:], kn[:, t, :], 0.5, acc_p[t][:], ALU.add, ALU.mult)
-            nc.vector.scalar_tensor_tensor(terms[2][:], over[:], -1.0 / 16.0, prow[:, t * P : (t + 1) * P], ALU.mult, ALU.mult)
-            back = psum.tile([P, P], F32, name="back%d" % t, tag="b01%d" % t)
+            nc.scalar.activation(over[t][:], sum_r[t][:], ACT.Relu, scale=-1.0, bias=neg_budg16[:, 0:1])
+        for t in range(2):
+            out_terms = [keep.tile([P, P], F32, name="out_term%d%d" % (t, i)) for i in range(3)]
+            nc.vector.scalar_tensor_tensor(out_terms[0][:], sum_u[t][:], -0.5, neg_half_m[:, t, :], ALU.mult, ALU.mult)
+            nc.vector.scalar_tensor_tensor(out_terms[1][:], neg_half_m[:, t, :], 0.5, sum_r[t][:], ALU.add, ALU.mult)
+            nc.vector.scalar_tensor_tensor(out_terms[2][:], over[t][:], -1.0 / 16.0, pen_row[:, t * P : (t + 1) * P], ALU.mult, ALU.mult)
+            out_sum = psum.tile([P, P], F32, name="out_sum%d" % t, tag=bank(VALUE, 1, t))
             for i in range(3):
-                nc.tensor.matmul(back[:], terms[i][:], ident[:], start=(i == 0), stop=(i == 2), is_transpose=True)
-            res = keep.tile([P, V], F32, name="res%d" % t)
-            nc.scalar.copy(res[:], back[:])
-            nc.sync.dma_start(out[t * P : (t + 1) * P, :], res[:])
+                nc.tensor.matmul(out_sum[:], out_terms[i][:], ident[:], start=(i == 0), stop=(i == 2), is_transpose=True)
+            result = shared.tile([P, V], F32, name="result%d" % t, offset=6144 + 512 * t, align_bytes=64)
+            nc.scalar.copy(result[:], out_sum[:])
+            nc.sync.dma_start(out[t * P : (t + 1) * P, :], result[:])

from contextlib import ExitStack

import concourse.mybir as mybir
from concourse.masks import make_identity

F32 = mybir.dt.float32
BF16 = mybir.dt.bfloat16
I32 = mybir.dt.int32
U32 = mybir.dt.uint32
U16 = mybir.dt.uint16
U8 = mybir.dt.uint8
FP8X4 = mybir.dt.float8_e4m3fn_x4
ALU = mybir.AluOpType
ACT = mybir.ActivationFunctionType

P = 128
K = 512
PACK = 4
T = 4096
S = 1024
D = 8
N = 256
V = 128
HALF = S // 2
VH = V // 2
PAIRS = D // 2
CAP = 30.0
VALUE, PRICE = 0, 1

FLOPS = 2 * K * 2 * N * S


def tile_picked_ypacng_sur_p_kernel(tc, x_words, x_scales, w1, w2, mult, budg, pen, offs, out):
    nc = tc.nc
    with ExitStack() as ctx:
        keep = ctx.enter_context(tc.tile_pool(name="keep", bufs=1))
        shared = ctx.enter_context(tc.tile_pool(name="shared", bufs=1))
        psum = ctx.enter_context(tc.psum_pool(name="psum", bufs=1))

        offsets = keep.tile([P, S // 16], U16, name="offsets")
        nc.sync.dma_start(offsets[:], offs)

        raw_value = keep.tile([P, PACK, N], F32, name="raw_value", tag="raw_value")
        nc.sync.dma_start(raw_value[:], w1.rearrange("(p j) n -> p j n", j=PACK))

        scale_table = keep.tile([P, T], U8, name="scale_table", tag="scale_table", align_bytes=64)
        x_scale = keep.tile([P, S], U8, name="x_scale", align_bytes=64)
        nc.vector.memset(scale_table[:].bitcast(I32), 0)
        nc.sync.dma_start(scale_table[0:P:8, :].bitcast(I32), x_scales[0].bitcast(I32))

        one = shared.tile([P, 1], F32, name="one", offset=0, align_bytes=64)
        floor = keep.tile([P, 1], F32, name="floor")
        nc.vector.memset(one[:], 1.0)
        cap = keep.tile([P, 1], F32, name="cap")
        nc.vector.tensor_scalar(cap[:], one[:], CAP, None, ALU.mult)
        nc.scalar.activation(floor[:], cap[:], ACT.Sigmoid, scale=-1.0)
        ident = keep.tile([P, P], F32, name="ident")
        make_identity(nc, ident[:])
        nc.vector.memset(x_scale[:].bitcast(I32), 0)
        word_table = shared.tile([P, T], U32, name="word_table", offset=0, align_bytes=64)
        nc.sync.dma_start(word_table[:].bitcast(I32), x_words[0].rearrange("p n t -> p (n t)").bitcast(I32))

        grouped = [
            keep.tile([P, N, PACK], BF16, name="grouped_value", align_bytes=64),
            shared.tile([P, N, PACK], BF16, name="grouped_price", offset=0, align_bytes=64),
        ]
        w_word = [keep.tile([P, N], U32, name="w_word%d" % a, align_bytes=64) for a in (VALUE, PRICE)]
        w_scale = [keep.tile([P, N], U8, name="w_scale%d" % a, align_bytes=64) for a in (VALUE, PRICE)]

        def quantise(a, cols):
            nc.vector.quantize_mx(
                out=w_word[a][:, cols].bitcast(FP8X4),
                scales=w_scale[a][:, cols],
                in_=grouped[a][:, cols, :].rearrange("p n j -> p (n j)"),
            )

        nc.scalar.copy(grouped[VALUE][:], raw_value[:].rearrange("p j n -> p n j"))
        mult_rows = keep.tile([P, 2, V], F32, name="mult_rows", tag="raw_value")
        nc.sync.dma_start(mult_rows[:], mult.rearrange("(t p) v -> p t v", p=P))

        picked_scale = keep.tile([P, S], U8, name="picked_scale", align_bytes=64)
        nc.vector.tensor_copy(picked_scale[:], scale_table[:].indirect(offsets[:]))
        for q in range(4):
            nc.sync.dma_start(x_scale[32 * q : 32 * q + 4, :].bitcast(I32), picked_scale[32 * q : 32 * q + 32 : 8, :].bitcast(I32))
        raw_price = keep.tile([P, PACK, N], F32, name="raw_price", tag="scale_table", align_bytes=64)
        nc.sync.dma_start(raw_price[:], w2.rearrange("(p j) n -> p j n", j=PACK))
        quantise(VALUE, slice(0, N))

        x_word = [keep.tile([P, HALF], U32, name="x_word%d" % h, align_bytes=64) for h in range(2)]
        for h in range(2):
            nc.vector.tensor_copy(x_word[h][:], word_table[:].indirect(offsets[:, h * (HALF // 16) : (h + 1) * (HALF // 16)]))

        for t in (1, 0):
            cols = slice(t * P, (t + 1) * P)
            nc.vector.tensor_copy(grouped[PRICE][:, cols, :], raw_price[:, :, cols].rearrange("p j n -> p n j"))
        for t in (1, 0):
            quantise(PRICE, slice(t * P, (t + 1) * P))

        budg_col = shared.tile([P, 1], F32, name="budg_col", offset=5120, align_bytes=64)
        pen_row = shared.tile([P, N], F32, name="pen_row", offset=4096, align_bytes=64)
        nc.sync.dma_start(pen_row[:], pen.rearrange("m o -> (m o)").partition_broadcast(P))
        with nc.allow_non_contiguous_dma(reason="one value a partition"):
            nc.sync.dma_start(budg_col[:], budg[0:1, :].rearrange("o v -> v o"))

        def bank(a, t, h):
            return "bank%d%d%d" % (a, t, h)

        mult_turned = psum.tile([P, 2, P], F32, name="mult_turned", tag=bank(PRICE, 0, 0))
        for t in range(2):
            nc.tensor.transpose(mult_turned[:, t, :], mult_rows[:, t, :], ident[:])
        neg_half_m = shared.tile([P, 2, P], F32, name="neg_half_m", offset=1024, align_bytes=64)
        nc.vector.tensor_scalar(neg_half_m[:], mult_turned[:], 0.3, -0.5, ALU.add, ALU.mult)
        m_rows = shared.tile([P, 2, V], F32, name="m_rows", offset=0, align_bytes=64)
        inv_m = keep.tile([P, 2, V], F32, name="inv_m")
        neg_budg16 = shared.tile([P, 1], F32, name="neg_budg16", offset=6144, align_bytes=64)
        nc.vector.tensor_scalar(m_rows[:], mult_rows[:], 0.3, None, ALU.add)
        nc.vector.reciprocal(inv_m[:], m_rows[:])
        nc.vector.tensor_scalar(neg_budg16[:], budg_col[:], -16.0, None, ALU.mult)

        chunks = [(t, h) for t in range(2) for h in range(2)]
        products = [(VALUE, t, h) for h in range(2) for t in range(2)] + [(PRICE, t, h) for t, h in reversed(chunks)]
        y = {}
        sig = {c: keep.tile([P, 2, HALF], F32, name="sig%d%d" % c) for c in chunks}
        for a, t, h in products:
            y[a, t, h] = psum.tile([P, HALF], F32, name="y%d%d%d" % (a, t, h), tag=bank(a, t, h))
            nc.tensor.matmul_mx(
                out=y[a, t, h][:],
                lhsT=w_word[a][:, t * P : (t + 1) * P].bitcast(FP8X4),
                lhsT_scale=w_scale[a][:, t * P : (t + 1) * P],
                rhs=x_word[h][:].bitcast(FP8X4),
                rhs_scale=x_scale[:, h * HALF : (h + 1) * HALF],
                start=True,
                stop=True,
            )
            nc.scalar.activation(sig[t, h][:, a, :], y[a, t, h][:], ACT.Sigmoid, scale=-1.0)

        whole = slice(0, HALF)
        first_pieces = [slice(0, HALF // 2), slice(HALF // 2, HALF)]
        log_sig = {c: keep.tile([P, 2, HALF], F32, name="log_sig%d%d" % c) for c in chunks}
        for c in chunks:
            for js in first_pieces if c == chunks[0] else [whole]:
                nc.scalar.activation(log_sig[c][:, :, js], sig[c][:, :, js], ACT.Ln, bias=floor[:, 0:1])

        neg_soft = {c: keep.tile([P, HALF], F32, name="neg_soft%d%d" % c) for c in chunks}
        neg_bid = {c: keep.tile([P, HALF], F32, name="neg_bid%d%d" % c) for c in chunks}
        neg_pri = [keep.tile([P, 2, HALF], F32, name="neg_pri%d" % t) for t in range(2)]
        neg_u = [keep.tile([P, 2, HALF], F32, name="neg_u%d" % t) for t in range(2)]

        def softplus(a, c, js):
            t, h = c
            dst = neg_soft[c][:, js] if a == VALUE else neg_pri[t][:, h, js]
            nc.vector.scalar_tensor_tensor(dst, y[a, t, h][:, js], -1.0, log_sig[c][:, a, js], ALU.mult, ALU.min)

        def bid(c):
            t, h = c
            nc.vector.scalar_tensor_tensor(
                neg_bid[c][:].rearrange("p (v d) -> p v d", d=D),
                neg_soft[c][:].rearrange("p (v d) -> p v d", d=D),
                -0.2,
                inv_m[:, t, h * VH : (h + 1) * VH].unsqueeze(2).to_broadcast([P, VH, D]),
                ALU.add,
                ALU.mult,
            )

        def margin(c, engine):
            t, h = c
            engine.tensor_tensor(neg_u[t][:, h, :], neg_bid[c][:], neg_pri[t][:, h, :], ALU.subtract)

        c0, c1, c2, c3 = chunks
        for js in first_pieces:
            softplus(VALUE, c0, js)
            softplus(PRICE, c0, js)
        bid(c0)
        margin(c0, nc.gpsimd)
        softplus(VALUE, c1, whole)
        softplus(PRICE, c1, whole)
        softplus(VALUE, c2, whole)
        bid(c1)
        margin(c1, nc.gpsimd)
        softplus(PRICE, c2, whole)
        softplus(VALUE, c3, whole)
        softplus(PRICE, c3, whole)
        bid(c2)
        bid(c3)
        margin(c2, nc.vector)
        margin(c3, nc.vector)

        sum_u = [psum.tile([P, P], F32, name="sum_u%d" % t, tag=bank(VALUE, 0, t)) for t in range(2)]
        sum_r = [psum.tile([P, P], F32, name="sum_r%d" % t, tag=bank(PRICE, 0, t)) for t in range(2)]
        for t in range(2):
            u_terms = keep.tile([P, D, V], F32, name="u_terms%d" % t)
            tanh_u = keep.tile([P, PAIRS, V, 2], F32, name="tanh_u%d" % t)
            r_terms = keep.tile([P, D, V], F32, name="r_terms%d" % t)
            neg_u_pairs = neg_u[t][:].rearrange("p h (v g e) -> p g (h v) e", g=PAIRS, e=2)
            neg_pri_pairs = neg_pri[t][:].rearrange("p h (v g e) -> p g (h v) e", g=PAIRS, e=2)
            u_terms_pairs = u_terms[:].rearrange("p (g e) v -> p g v e", e=2)
            r_terms_pairs = r_terms[:].rearrange("p (g e) v -> p g v e", e=2)

            def silu(gs, vs):
                nc.scalar.activation(u_terms_pairs[:, gs, vs, :], neg_u_pairs[:, gs, vs, :], ACT.Silu, scale=-4.0)

            def tanh(gs, vs):
                nc.scalar.activation(tanh_u[:, gs, vs, :], neg_u_pairs[:, gs, vs, :], ACT.Tanh, scale=-2.0)

            def add_up(acc, terms, d0, d1):
                for d in range(d0, d1):
                    nc.tensor.matmul(acc[:], terms[:, d, :], ident[:], start=(d == 0), stop=(d == D - 1), is_transpose=True)

            def payments(g):
                nc.vector.scalar_tensor_tensor(r_terms_pairs[:, g, :, :], tanh_u[:, g, :, :], 1.0, neg_pri_pairs[:, g, :, :], ALU.add, ALU.mult)
                add_up(sum_r[t], r_terms, 2 * g, 2 * g + 2)

            every_pair = slice(0, PAIRS)
            if t == 0:
                for h in range(2):
                    silu(every_pair, slice(h * VH, (h + 1) * VH))
                    tanh(every_pair, slice(h * VH, (h + 1) * VH))
                add_up(sum_u[t], u_terms, 0, D)
                for g in range(PAIRS):
                    payments(g)
            else:
                tanh(every_pair, slice(0, VH))
                silu(every_pair, slice(0, VH))
                for g0, g1 in [(0, 2), (2, 3), (3, 4)]:
                    tanh(slice(g0, g1), slice(VH, V))
                    silu(slice(g0, g1), slice(VH, V))
                    for g in range(g0, g1):
                        payments(g)
                    add_up(sum_u[t], u_terms, 2 * g0, 2 * g1)

        over = [keep.tile([P, P], F32, name="over%d" % t) for t in range(2)]
        for t in range(2):
            nc.scalar.activation(over[t][:], sum_r[t][:], ACT.Relu, scale=-1.0, bias=neg_budg16[:, 0:1])
        for t in range(2):
            out_terms = [keep.tile([P, P], F32, name="out_term%d%d" % (t, i)) for i in range(3)]
            nc.vector.scalar_tensor_tensor(out_terms[0][:], sum_u[t][:], -0.5, neg_half_m[:, t, :], ALU.mult, ALU.mult)
            nc.vector.scalar_tensor_tensor(out_terms[1][:], neg_half_m[:, t, :], 0.5, sum_r[t][:], ALU.add, ALU.mult)
            nc.vector.scalar_tensor_tensor(out_terms[2][:], over[t][:], -1.0 / 16.0, pen_row[:, t * P : (t + 1) * P], ALU.mult, ALU.mult)
            out_sum = psum.tile([P, P], F32, name="out_sum%d" % t, tag=bank(VALUE, 1, t))
            for i in range(3):
                nc.tensor.matmul(out_sum[:], out_terms[i][:], ident[:], start=(i == 0), stop=(i == 2), is_transpose=True)
            result = shared.tile([P, V], F32, name="result%d" % t, offset=6144 + 512 * t, align_bytes=64)
            nc.scalar.copy(result[:], out_sum[:])
            nc.sync.dma_start(out[t * P : (t + 1) * P, :], result[:])
